import numpy as np
import ml_dtypes

BF16 = ml_dtypes.bfloat16


def bf(x):
    return np.asarray(x, np.float32).astype(BF16)


def f32(x):
    return np.asarray(x, np.float32)


def f64(x):
    return np.asarray(x).astype(np.float64)


def striped(idx):
    return np.tile(idx.reshape(-1, 16).T, (8, 1))


S, K, M, N, D, V = 512, 128, 512, 256, 2, 128


def setup_inputs():
    return {"table": bf(np.random.standard_normal((K, S))), "w": bf(np.random.standard_normal((D, K, M)) / np.sqrt(D * K)), "b": f32(0.5 * np.random.standard_normal((M, 1))), "offs": striped(np.random.permutation(np.tile(np.arange(S), 2))[:N])}


def reference(table, w, b, offs):
    idx = offs[:16].T.reshape(-1)
    x = f64(table)[:, idx]
    y = sum(f64(w)[t].T @ x[:, t * V : (t + 1) * V] for t in range(D))
    return np.tanh(y + f64(b))

@@ -1,0 +1,48 @@
+import concourse.mybir as mybir
+
+BF16, F32, U16 = mybir.dt.bfloat16, mybir.dt.float32, mybir.dt.uint16
+TANH = mybir.ActivationFunctionType.Tanh
+
+P = 128
+NODES = 512
+ENDS = 2
+EDGES = 128
+OUT_FEATURES = 512
+BLOCKS = OUT_FEATURES // P
+LIST_COLUMNS = EDGES // 16
+
+FLOPS = 2 * OUT_FEATURES * EDGES * ENDS * P
+
+
+def tile_gather_matmul_kernel(tc, table, w, b, offs, out):
+    nc = tc.nc
+    with (
+        tc.tile_pool(name="held", bufs=1) as held,
+        tc.tile_pool(name="results", bufs=BLOCKS) as results,
+        tc.psum_pool(name="psum", bufs=BLOCKS) as psum,
+    ):
+        offsets = held.tile([P, ENDS * LIST_COLUMNS], U16, name="offsets")
+        nc.sync.dma_start(offsets[:], offs)
+        nodes = held.tile([P, NODES], BF16, name="nodes")
+        nc.scalar.dma_start(nodes[:], table)
+        weights = [held.tile([P, OUT_FEATURES], BF16, name=f"weights{t}") for t in range(ENDS)]
+        nc.sync.dma_start(weights[0][:], w[0, :, :])
+        nc.scalar.dma_start(weights[1][:], w[1, :, :])
+        bias = held.tile([P, BLOCKS], F32, name="bias")
+        with nc.allow_non_contiguous_dma(reason="512 single float32 values, one to a partition and block"):
+            nc.gpsimd.dma_start(bias[:], b.rearrange("(a p) o -> p (a o)", p=P))
+
+        for a in range(BLOCKS):
+            bank = psum.tile([P, EDGES], F32, name="bank")
+            for t in range(ENDS):
+                picked = nodes[:].indirect(offsets[:, t * LIST_COLUMNS : (t + 1) * LIST_COLUMNS])
+                nc.tensor.matmul(
+                    bank[:],
+                    weights[t][:, a * P : (a + 1) * P],
+                    picked,
+                    start=(t == 0),
+                    stop=(t == ENDS - 1),
+                )
+            result = results.tile([P, EDGES], F32, name="result")
+            nc.scalar.activation(result[:], bank[:], TANH, bias=bias[:, a : a + 1])
+            nc.sync.dma_start(out[a * P : (a + 1) * P, :], result[:])

@@ -19,7 +19,7 @@ def tile_gather_matmul_kernel(tc, table, w, b, offs, out):
     with (
         tc.tile_pool(name="held", bufs=1) as held,
         tc.tile_pool(name="results", bufs=BLOCKS) as results,
-        tc.psum_pool(name="psum", bufs=BLOCKS) as psum,
+        tc.psum_pool(name="psum", bufs=1) as psum,
     ):
         offsets = held.tile([P, ENDS * LIST_COLUMNS], U16, name="offsets")
         nc.sync.dma_start(offsets[:], offs)
@@ -30,19 +30,25 @@ def tile_gather_matmul_kernel(tc, table, w, b, offs, out):
         nc.scalar.dma_start(weights[1][:], w[1, :, :])
         bias = held.tile([P, BLOCKS], F32, name="bias")
         with nc.allow_non_contiguous_dma(reason="512 single float32 values, one to a partition and block"):
-            nc.gpsimd.dma_start(bias[:], b.rearrange("(a p) o -> p (a o)", p=P))
+            nc.scalar.dma_start(bias[:], b.rearrange("(a p) o -> p (a o)", p=P))
 
-        for a in range(BLOCKS):
-            bank = psum.tile([P, EDGES], F32, name="bank")
-            for t in range(ENDS):
-                picked = nodes[:].indirect(offsets[:, t * LIST_COLUMNS : (t + 1) * LIST_COLUMNS])
+        scratch = held.tile([P, 1], F32, name="scratch")
+        nc.vector.memset(scratch[:], 0.0)
+        nc.scalar.activation(scratch[:], scratch[:], TANH)
+
+        banks = [psum.tile([P, EDGES], F32, name=f"bank{a}") for a in range(BLOCKS)]
+        for t in range(ENDS):
+            picked = nodes[:].indirect(offsets[:, t * LIST_COLUMNS : (t + 1) * LIST_COLUMNS])
+            for a in range(BLOCKS):
                 nc.tensor.matmul(
-                    bank[:],
+                    banks[a][:],
                     weights[t][:, a * P : (a + 1) * P],
                     picked,
                     start=(t == 0),
                     stop=(t == ENDS - 1),
                 )
+
+        for a in range(BLOCKS):
             result = results.tile([P, EDGES], F32, name="result")
-            nc.scalar.activation(result[:], bank[:], TANH, bias=bias[:, a : a + 1])
+            nc.scalar.activation(result[:], banks[a][:], TANH, bias=bias[:, a : a + 1])
             nc.sync.dma_start(out[a * P : (a + 1) * P, :], result[:])

@@ -10,6 +10,7 @@ EDGES = 128
 OUT_FEATURES = 512
 BLOCKS = OUT_FEATURES // P
 LIST_COLUMNS = EDGES // 16
+WARM_MATMULS = 16
 
 FLOPS = 2 * OUT_FEATURES * EDGES * ENDS * P
 
@@ -32,9 +33,13 @@ def tile_gather_matmul_kernel(tc, table, w, b, offs, out):
         with nc.allow_non_contiguous_dma(reason="512 single float32 values, one to a partition and block"):
             nc.scalar.dma_start(bias[:], b.rearrange("(a p) o -> p (a o)", p=P))
 
+        zeros = held.tile([P, P], BF16, name="zeros")
+        nc.vector.memset(zeros[:], 0.0)
+        warm_bank = psum.tile([P, P], F32, name="warm_bank")
+        for i in range(WARM_MATMULS):
+            nc.tensor.matmul(warm_bank[:], zeros[:], zeros[:], start=True, stop=True)
         scratch = held.tile([P, 1], F32, name="scratch")
-        nc.vector.memset(scratch[:], 0.0)
-        nc.scalar.activation(scratch[:], scratch[:], TANH)
+        nc.scalar.activation(scratch[:], zeros[:, 0:1], TANH)
 
         banks = [psum.tile([P, EDGES], F32, name=f"bank{a}") for a in range(BLOCKS)]
         for t in range(ENDS):

@@ -10,7 +10,6 @@ EDGES = 128
 OUT_FEATURES = 512
 BLOCKS = OUT_FEATURES // P
 LIST_COLUMNS = EDGES // 16
-WARM_MATMULS = 16
 
 FLOPS = 2 * OUT_FEATURES * EDGES * ENDS * P
 
@@ -29,17 +28,13 @@ def tile_gather_matmul_kernel(tc, table, w, b, offs, out):
         weights = [held.tile([P, OUT_FEATURES], BF16, name=f"weights{t}") for t in range(ENDS)]
         nc.sync.dma_start(weights[0][:], w[0, :, :])
         nc.scalar.dma_start(weights[1][:], w[1, :, :])
-        bias = held.tile([P, BLOCKS], F32, name="bias")
-        with nc.allow_non_contiguous_dma(reason="512 single float32 values, one to a partition and block"):
-            nc.scalar.dma_start(bias[:], b.rearrange("(a p) o -> p (a o)", p=P))
+        bias = [held.tile([P, 1], F32, name=f"bias{a}") for a in range(BLOCKS)]
+        for a in range(BLOCKS):
+            nc.sync.dma_start(bias[a][:], b[a * P : (a + 1) * P, :])
 
-        zeros = held.tile([P, P], BF16, name="zeros")
-        nc.vector.memset(zeros[:], 0.0)
-        warm_bank = psum.tile([P, P], F32, name="warm_bank")
-        for i in range(WARM_MATMULS):
-            nc.tensor.matmul(warm_bank[:], zeros[:], zeros[:], start=True, stop=True)
         scratch = held.tile([P, 1], F32, name="scratch")
-        nc.scalar.activation(scratch[:], zeros[:, 0:1], TANH)
+        nc.vector.memset(scratch[:], 0.0)
+        nc.scalar.activation(scratch[:], scratch[:], TANH)
 
         banks = [psum.tile([P, EDGES], F32, name=f"bank{a}") for a in range(BLOCKS)]
         for t in range(ENDS):
@@ -55,5 +50,5 @@ def tile_gather_matmul_kernel(tc, table, w, b, offs, out):
 
         for a in range(BLOCKS):
             result = results.tile([P, EDGES], F32, name="result")
-            nc.scalar.activation(result[:], banks[a][:], TANH, bias=bias[:, a : a + 1])
+            nc.scalar.activation(result[:], banks[a][:], TANH, bias=bias[a][:])
             nc.sync.dma_start(out[a * P : (a + 1) * P, :], result[:])

@@ -21,12 +21,12 @@ def tile_gather_matmul_kernel(tc, table, w, b, offs, out):
         tc.tile_pool(name="results", bufs=BLOCKS) as results,
         tc.psum_pool(name="psum", bufs=1) as psum,
     ):
-        offsets = held.tile([P, ENDS * LIST_COLUMNS], U16, name="offsets")
-        nc.sync.dma_start(offsets[:], offs)
         nodes = held.tile([P, NODES], BF16, name="nodes")
         nc.scalar.dma_start(nodes[:], table)
         weights = [held.tile([P, OUT_FEATURES], BF16, name=f"weights{t}") for t in range(ENDS)]
         nc.sync.dma_start(weights[0][:], w[0, :, :])
+        offsets = held.tile([P, ENDS * LIST_COLUMNS], U16, name="offsets")
+        nc.sync.dma_start(offsets[:], offs)
         nc.scalar.dma_start(weights[1][:], w[1, :, :])
         bias = [held.tile([P, 1], F32, name=f"bias{a}") for a in range(BLOCKS)]
         for a in range(BLOCKS):

@@ -37,13 +37,12 @@ def tile_gather_matmul_kernel(tc, table, w, b, offs, out):
         nc.scalar.activation(scratch[:], scratch[:], TANH)
 
         banks = [psum.tile([P, EDGES], F32, name=f"bank{a}") for a in range(BLOCKS)]
-        for t in range(ENDS):
-            picked = nodes[:].indirect(offsets[:, t * LIST_COLUMNS : (t + 1) * LIST_COLUMNS])
-            for a in range(BLOCKS):
+        for a in range(BLOCKS):
+            for t in range(ENDS):
                 nc.tensor.matmul(
                     banks[a][:],
                     weights[t][:, a * P : (a + 1) * P],
-                    picked,
+                    nodes[:].indirect(offsets[:, t * LIST_COLUMNS : (t + 1) * LIST_COLUMNS]),
                     start=(t == 0),
                     stop=(t == ENDS - 1),
                 )

@@ -10,6 +10,8 @@ EDGES = 128
 OUT_FEATURES = 512
 BLOCKS = OUT_FEATURES // P
 LIST_COLUMNS = EDGES // 16
+LOADS = 2
+BLOCKS_A_LOAD = BLOCKS // LOADS
 
 FLOPS = 2 * OUT_FEATURES * EDGES * ENDS * P
 
@@ -23,11 +25,13 @@ def tile_gather_matmul_kernel(tc, table, w, b, offs, out):
     ):
         nodes = held.tile([P, NODES], BF16, name="nodes")
         nc.scalar.dma_start(nodes[:], table)
-        weights = [held.tile([P, OUT_FEATURES], BF16, name=f"weights{t}") for t in range(ENDS)]
-        nc.sync.dma_start(weights[0][:], w[0, :, :])
+        columns = BLOCKS_A_LOAD * P
+        weights = [held.tile([P, ENDS, columns], BF16, name=f"weights{h}") for h in range(LOADS)]
+        by_feature = w.rearrange("t k m -> k t m")
+        nc.sync.dma_start(weights[0][:], by_feature[:, :, 0:columns])
         offsets = held.tile([P, ENDS * LIST_COLUMNS], U16, name="offsets")
         nc.sync.dma_start(offsets[:], offs)
-        nc.scalar.dma_start(weights[1][:], w[1, :, :])
+        nc.scalar.dma_start(weights[1][:], by_feature[:, :, columns : 2 * columns])
         bias = [held.tile([P, 1], F32, name=f"bias{a}") for a in range(BLOCKS)]
         for a in range(BLOCKS):
             nc.sync.dma_start(bias[a][:], b[a * P : (a + 1) * P, :])
@@ -38,10 +42,11 @@ def tile_gather_matmul_kernel(tc, table, w, b, offs, out):
 
         banks = [psum.tile([P, EDGES], F32, name=f"bank{a}") for a in range(BLOCKS)]
         for a in range(BLOCKS):
+            h, c = divmod(a, BLOCKS_A_LOAD)
             for t in range(ENDS):
                 nc.tensor.matmul(
                     banks[a][:],
-                    weights[t][:, a * P : (a + 1) * P],
+                    weights[h][:, t, c * P : (c + 1) * P],
                     nodes[:].indirect(offsets[:, t * LIST_COLUMNS : (t + 1) * LIST_COLUMNS]),
                     start=(t == 0),
                     stop=(t == ENDS - 1),

@@ -12,6 +12,7 @@ BLOCKS = OUT_FEATURES // P
 LIST_COLUMNS = EDGES // 16
 LOADS = 2
 BLOCKS_A_LOAD = BLOCKS // LOADS
+PROBE_COLUMNS = 512
 
 FLOPS = 2 * OUT_FEATURES * EDGES * ENDS * P
 
@@ -36,7 +37,7 @@ def tile_gather_matmul_kernel(tc, table, w, b, offs, out):
         for a in range(BLOCKS):
             nc.sync.dma_start(bias[a][:], b[a * P : (a + 1) * P, :])
 
-        scratch = held.tile([P, 1], F32, name="scratch")
+        scratch = held.tile([P, PROBE_COLUMNS], F32, name="scratch")
         nc.vector.memset(scratch[:], 0.0)
         nc.scalar.activation(scratch[:], scratch[:], TANH)
 

import concourse.mybir as mybir

BF16, F32, U16 = mybir.dt.bfloat16, mybir.dt.float32, mybir.dt.uint16
TANH = mybir.ActivationFunctionType.Tanh

P = 128
NODES = 512
ENDS = 2
EDGES = 128
OUT_FEATURES = 512
BLOCKS = OUT_FEATURES // P
LIST_COLUMNS = EDGES // 16
LOADS = 2
BLOCKS_A_LOAD = BLOCKS // LOADS
PROBE_COLUMNS = 512

FLOPS = 2 * OUT_FEATURES * EDGES * ENDS * P


def tile_gather_matmul_kernel(tc, table, w, b, offs, out):
    nc = tc.nc
    with (
        tc.tile_pool(name="held", bufs=1) as held,
        tc.tile_pool(name="results", bufs=BLOCKS) as results,
        tc.psum_pool(name="psum", bufs=1) as psum,
    ):
        nodes = held.tile([P, NODES], BF16, name="nodes")
        nc.scalar.dma_start(nodes[:], table)
        columns = BLOCKS_A_LOAD * P
        weights = [held.tile([P, ENDS, columns], BF16, name=f"weights{h}") for h in range(LOADS)]
        by_feature = w.rearrange("t k m -> k t m")
        nc.sync.dma_start(weights[0][:], by_feature[:, :, 0:columns])
        offsets = held.tile([P, ENDS * LIST_COLUMNS], U16, name="offsets")
        nc.sync.dma_start(offsets[:], offs)
        nc.scalar.dma_start(weights[1][:], by_feature[:, :, columns : 2 * columns])
        bias = [held.tile([P, 1], F32, name=f"bias{a}") for a in range(BLOCKS)]
        for a in range(BLOCKS):
            nc.sync.dma_start(bias[a][:], b[a * P : (a + 1) * P, :])

        scratch = held.tile([P, PROBE_COLUMNS], F32, name="scratch")
        nc.vector.memset(scratch[:], 0.0)
        nc.scalar.activation(scratch[:], scratch[:], TANH)

        banks = [psum.tile([P, EDGES], F32, name=f"bank{a}") for a in range(BLOCKS)]
        for a in range(BLOCKS):
            h, c = divmod(a, BLOCKS_A_LOAD)
            for t in range(ENDS):
                nc.tensor.matmul(
                    banks[a][:],
                    weights[h][:, t, c * P : (c + 1) * P],
                    nodes[:].indirect(offsets[:, t * LIST_COLUMNS : (t + 1) * LIST_COLUMNS]),
                    start=(t == 0),
                    stop=(t == ENDS - 1),
                )

        for a in range(BLOCKS):
            result = results.tile([P, EDGES], F32, name="result")
            nc.scalar.activation(result[:], banks[a][:], TANH, bias=bias[a][:])
            nc.sync.dma_start(out[a * P : (a + 1) * P, :], result[:])
